import numpy as np
import ml_dtypes


def mxq(x, axis, fmt="e4m3"):
    dtype, down = {"e4m3": (ml_dtypes.float8_e4m3fn, 7), "e5m2": (ml_dtypes.float8_e5m2, 14)}[fmt]
    v = np.moveaxis(np.asarray(x, np.float32).astype(ml_dtypes.bfloat16).astype(np.float64), axis, -1)
    blocks = v.reshape(v.shape[:-1] + (-1, 32))
    amax = np.abs(blocks).max(-1, keepdims=True)
    byte = np.maximum(np.where(amax > 0, np.frexp(amax)[1] - 1 + 127, 0) - down, 1)
    scale = np.exp2(byte - 127.0)
    codes = (blocks / scale).astype(np.float32).astype(dtype).astype(np.float64)
    return np.moveaxis((codes * scale).reshape(v.shape), -1, axis)


WIDE = False


def mx_kscale(k):
    if not WIDE:
        return np.ones(k)
    levels = np.array([10, -10, 5, -5, 0])
    if k % 512:
        return np.exp2(np.random.permutation(np.resize(levels, k // 32))).repeat(32)
    a = np.empty((k // 512, 16))
    for p in range(k // 512):
        a[p, :8] = np.random.permutation(np.resize(levels, 8))
        for g in range(8):
            far = levels[np.abs(levels - a[p, g]) >= 10]
            a[p, g + 8] = far[np.random.randint(len(far))]
    return np.exp2(a.ravel()).repeat(32)


def f64(x):
    return np.asarray(x).astype(np.float64)


def striped(idx):
    return np.tile(idx.reshape(-1, 16).T, (8, 1)).astype(np.uint16)


def unstriped(offs):
    return offs[:16].T.reshape(-1).astype(np.int64)


def striped8(idx):
    return np.concatenate([x.reshape(-1, 16).T for x in idx]).astype(np.uint16)


def runs(offs, k):
    lists = np.stack([offs[16 * r : 16 * r + 16].T.reshape(-1) for r in range(8)]).astype(np.int64)
    return lists[np.arange(k) % 512 // 64]


def pack_weight(w):
    k, n = w.shape
    w = f64(np.asarray(w, np.float32).astype(ml_dtypes.bfloat16)).reshape(k // 32, 32, n)
    amax = np.abs(w).max(1)
    byte = np.clip(np.where(amax > 0, np.frexp(amax)[1] - 1 + 127 - 7, 1), 1, 254)
    scaled = (w * np.exp2(127.0 - byte)[:, None, :]).reshape(k, n).astype(np.float32)
    words = np.ascontiguousarray(scaled.reshape(k // 512, 128, 4, n).transpose(0, 1, 3, 2)).astype(ml_dtypes.float8_e4m3fn).view(np.uint8)
    return words, np.ascontiguousarray(byte.astype(np.uint8).reshape(k // 512, 16, n))


def unpack_weight(words, scales):
    g, p, n, _ = words.shape
    vals = np.ascontiguousarray(words).view(ml_dtypes.float8_e4m3fn).astype(np.float64) * np.repeat(np.exp2(scales.astype(np.float64) - 127.0), 8, axis=1)[..., None]
    return vals.transpose(0, 1, 3, 2).reshape(g * 512, n)


K, T, S, V, G, H, U = 512, 1024, 512, 512, 2048, 512, 1024


def setup_inputs():
    n = np.random.standard_normal
    s = mx_kscale(K)[:, None]
    u = mx_kscale(S)
    packed_xT = pack_weight(n((K, T)) * s)
    packed_dT = pack_weight(n((K, G)) / s)
    return {
        "x_words": packed_xT[0],
        "x_scales": packed_xT[1],
        "d_words": packed_dT[0],
        "d_scales": packed_dT[1],
        "w1": (n((K, H)) / np.sqrt(K) / s).astype(np.float32),
        "mem": n((H, U)).astype(np.float32),
        "ga": (np.random.uniform(0.5, 1.5, (H, 1)) * u[:, None]).astype(np.float32),
        "gb": (np.random.uniform(0.5, 1.5, (H, 1)) / u[:, None]).astype(np.float32),
        "offs": striped(np.random.permutation(T)[:S]),
        "k1": striped8(np.random.randint(0, G, (8, H))),
        "two": striped(np.random.permutation(T)[:V]),
        "n1": striped8(np.stack([np.random.permutation(S) for _ in range(8)])),
        "n2": striped8(np.stack([np.random.permutation(U)[:V] for _ in range(8)])),
        "n3": striped8(np.stack([np.random.permutation(U) for _ in range(8)])),
    }


def reference(x_words, x_scales, d_words, d_scales, w1, mem, ga, gb, offs, k1, two, n1, n2, n3):
    d_k1 = unpack_weight(d_words, d_scales)[np.arange(K)[:, None], runs(k1, K)]
    xq = unpack_weight(x_words, x_scales)[:, unstriped(offs)]
    a = 0.0625 * (d_k1.T @ xq)
    z = f64(ga) * (a / (np.abs(a[np.arange(H)[:, None], runs(n1, H)]) + 0.5))
    x_two = unpack_weight(x_words, x_scales)[:, unstriped(two)]
    b = mxq(f64(w1), 0, "e4m3").T @ x_two
    pg = f64(mem).copy()
    pg[np.arange(H)[:, None], runs(n2, H)] = b
    z2 = f64(gb) * pg
    s = 0.0625 * ((mxq(z, 0, "e4m3").T @ mxq(z2, 0, "e4m3")))
    st = s - (s[np.arange(S)[:, None], runs(n3, S)])
    return st - (0.5 * (st[np.arange(S)[:, None], runs(n3, S)]))

@@ -1,0 +1,230 @@
+from contextlib import ExitStack
+
+import concourse.mybir as mybir
+
+K, T, S, V, G, H, U = 512, 1024, 512, 512, 2048, 512, 1024
+FLOPS = 2 * K * H * S + 2 * K * H * V + 2 * H * S * U
+
+F32 = mybir.dt.float32
+BF16 = mybir.dt.bfloat16
+I32 = mybir.dt.int32
+U32 = mybir.dt.uint32
+U16 = mybir.dt.uint16
+U8 = mybir.dt.uint8
+FP8X4 = mybir.dt.float8_e4m3fn_x4
+ACT = mybir.ActivationFunctionType
+ALU = mybir.AluOpType
+
+P = 128
+PACK = 4
+BANK = 512
+
+
+def tile_picked_ckqnormpagetwice_none_p_kernel(
+    tc, x_words, x_scales, d_words, d_scales, w1, mem, ga, gb, offs, k1, two, n1, n2, n3, out
+):
+    nc = tc.nc
+    with ExitStack() as ctx:
+        keep = ctx.enter_context(tc.tile_pool(name="keep", bufs=1))
+        ring = ctx.enter_context(tc.tile_pool(name="ring", bufs=3))
+        psum = ctx.enter_context(tc.psum_pool(name="psum", bufs=1))
+
+        def load_list(src, name):
+            tile = keep.tile(list(src.shape), U16, name=name)
+            nc.sync.dma_start(tile[:], src)
+            return tile
+
+        k1_list = load_list(k1, "k1_list")
+        d_scale_table = keep.tile([P, G], U8, align_bytes=64)
+        nc.sync.dma_start(
+            d_scale_table[:].bitcast(I32), d_scales[0].bitcast(I32).unsqueeze(1).to_broadcast([16, 8, G // 4])
+        )
+        two_list = load_list(two, "two_list")
+        offs_list = load_list(offs, "offs_list")
+        x_word_table = keep.tile([P, T], U32, align_bytes=64)
+        nc.sync.dma_start(x_word_table[:].bitcast(I32), x_words[0].rearrange("p n t -> p (n t)").bitcast(I32))
+        w_raw = keep.tile([P, PACK, H], F32)
+        nc.sync.dma_start(w_raw[:], w1.rearrange("(p j) c -> p j c", j=PACK))
+        x_scale_table = keep.tile([P, T], U8, align_bytes=64)
+        for q in range(4):
+            nc.sync.dma_start(
+                x_scale_table[32 * q : 32 * q + 32, :].bitcast(I32),
+                x_scales[0, 4 * q : 4 * q + 4, :].bitcast(I32).unsqueeze(0).to_broadcast([8, 4, T // 4]),
+            )
+        d_word_table = keep.tile([P, G], U32, align_bytes=64)
+        nc.sync.dma_start(d_word_table[:].bitcast(I32), d_words[0].rearrange("p n t -> p (n t)").bitcast(I32))
+        n2_list = load_list(n2, "n2_list")
+        mem_rows = mem.rearrange("(p t) w -> t p w", t=PACK)
+        pages = []
+        for t in range(PACK):
+            page = keep.tile([P, U], F32, name="page%d" % t)
+            nc.sync.dma_start(page[:], mem_rows[t])
+            pages.append(page)
+        n1_list = load_list(n1, "n1_list")
+        ga_cols = keep.tile([P, PACK], F32)
+        gb_cols = keep.tile([P, PACK], F32)
+        nc.sync.dma_start(ga_cols[:], ga.rearrange("(p t) o -> p (t o)", t=PACK))
+        nc.sync.dma_start(gb_cols[:], gb.rearrange("(p t) o -> p (t o)", t=PACK))
+        n3_list = load_list(n3, "n3_list")
+
+        def gather(table, offsets, dtype, name):
+            picked = keep.tile([P, S], dtype, name=name, align_bytes=64)
+            nc.vector.tensor_copy(picked[:], table[:].indirect(offsets[:]))
+            return picked
+
+        d_scales_picked = gather(d_scale_table, k1_list, U8, "d_scales_picked")
+        d_scales_dealt = keep.tile([P, H], U8, align_bytes=64)
+        nc.vector.tensor_copy(
+            d_scales_dealt[:].rearrange("p (t m) -> p m t", t=PACK),
+            d_scales_picked[:].rearrange("p (m t) -> p m t", t=PACK),
+        )
+        d_plane = keep.tile([P, H], U8, align_bytes=64)
+        nc.vector.tensor_copy(d_plane[:].bitcast(I32), d_scales_dealt[:].bitcast(I32))
+        for r in range(1, 4):
+            nc.scalar.dma_start(d_plane[r:P:32, :].bitcast(I32), d_scales_dealt[8 * r : P : 32, :].bitcast(I32))
+        two_words = gather(x_word_table, two_list, U32, "two_words")
+        offs_words = gather(x_word_table, offs_list, U32, "offs_words")
+        two_scales = gather(x_scale_table, two_list, U8, "two_scales")
+        offs_scales = gather(x_scale_table, offs_list, U8, "offs_scales")
+
+        w_grouped = keep.tile([P, PACK * H], BF16, align_bytes=64)
+        nc.scalar.copy(
+            w_grouped[:].rearrange("p (t m j) -> p m t j", t=PACK, j=PACK),
+            w_raw[:].rearrange("p j (m t) -> p m t j", t=PACK),
+        )
+        w_codes = keep.tile([P, H], U32, align_bytes=64)
+        w_plane = keep.tile([P, H], U8, align_bytes=64)
+        nc.vector.quantize_mx(out=w_codes[:].bitcast(FP8X4), scales=w_plane[:], in_=w_grouped[:])
+
+        d_words_picked = gather(d_word_table, k1_list, U32, "d_words_picked")
+        d_codes = keep.tile([P, H], U32, align_bytes=64)
+        nc.vector.tensor_copy(
+            d_codes[:].rearrange("p (t m) -> p m t", t=PACK),
+            d_words_picked[:].rearrange("p (m t) -> p m t", t=PACK),
+        )
+
+        def product(bank, codes, plane, t, moving_codes, moving_plane):
+            cols = slice(t * P, (t + 1) * P)
+            nc.tensor.matmul_mx(
+                out=bank[:],
+                lhsT=codes[:, cols].bitcast(FP8X4),
+                lhsT_scale=plane[:, cols],
+                rhs=moving_codes.bitcast(FP8X4),
+                rhs_scale=moving_plane,
+                start=True,
+                stop=True,
+            )
+
+        b_rows = keep.tile([P, PACK, V], F32)
+        for t in range(PACK):
+            b_bank = psum.tile([P, BANK], F32, name="b_bank%d" % t, tag="second%d" % t)
+            product(b_bank, w_codes, w_plane, t, two_words[:], two_scales[:])
+            nc.scalar.copy(b_rows[:, t, :], b_bank[:])
+        for t in range(PACK):
+            nc.vector.tensor_copy(pages[t][:].indirect(n2_list[:]), b_rows[:, t, :])
+
+        a_banks = []
+        logs = []
+        for t in range(PACK):
+            a_bank = psum.tile([P, BANK], F32, name="a_bank%d" % t, tag="first%d" % t)
+            product(a_bank, d_codes, d_plane, t, offs_words[:], offs_scales[:])
+            log_tile = keep.tile([P, 2 * S], F32, name="log_tile%d" % t, tag="shared%d" % t, align_bytes=64)
+            nc.scalar.activation(log_tile[:, S:], a_bank[:], ACT.Abs)
+            a_banks.append(a_bank)
+            logs.append(log_tile)
+        for t in range(PACK):
+            nc.scalar.activation(logs[t][:, :S], logs[t][:, S:], ACT.Ln, bias=8.0)
+        inverse = keep.tile([P, PACK, S], F32)
+        for t in range(PACK):
+            nc.scalar.activation(inverse[:, t, :], logs[t][:].indirect(n1_list[:]), ACT.Exp, scale=-1.0)
+        z_planes = keep.tile([P, PACK, S], BF16, align_bytes=64)
+        for t in range(PACK):
+            nc.vector.scalar_tensor_tensor(
+                z_planes[:, t, :], a_banks[t][:], ga_cols[:, t : t + 1], inverse[:, t, :], ALU.mult, ALU.mult
+            )
+
+        z_grouped = keep.tile([P, PACK, P, PACK], BF16, align_bytes=64)
+        z_codes = keep.tile([P, S], U32, align_bytes=64)
+        z_plane = keep.tile([P, S], U8, align_bytes=64)
+        z_dealt = z_planes[:].rearrange("p t (c m) -> p m c t", m=PACK)
+
+        def interleave_z(m):
+            nc.vector.tensor_copy(z_grouped[:, m], z_dealt[:, m])
+
+        def quantize_z(m):
+            cols = slice(m * P, (m + 1) * P)
+            nc.vector.quantize_mx(
+                out=z_codes[:, cols].bitcast(FP8X4),
+                scales=z_plane[:, cols],
+                in_=z_grouped[:, m].rearrange("p c t -> p (c t)"),
+            )
+
+        z2_codes = keep.tile([P, U], U32, align_bytes=64)
+        z2_plane = keep.tile([P, U], U8, align_bytes=64)
+        z2_grouped = []
+        interleave_z(0)
+        for h in range(2):
+            z2_planes = keep.tile([P, PACK, BANK], BF16, name="z2_planes%d" % h, tag="shared%d" % (3 - h), align_bytes=64)
+            for t in range(PACK):
+                nc.scalar.activation(
+                    z2_planes[:, t, :], pages[t][:, h * BANK : (h + 1) * BANK], ACT.Copy, scale=gb_cols[:, t : t + 1]
+                )
+            grouped = keep.tile([P, BANK, PACK], BF16, name="z2_grouped%d" % h, align_bytes=64)
+            nc.vector.tensor_copy(
+                grouped[:].rearrange("p (c i) t -> p c t i", i=4),
+                z2_planes[:].rearrange("p t (c i) -> p c t i", i=4),
+            )
+            z2_grouped.append(grouped)
+        quantize_z(0)
+        for h in range(2):
+            cols = slice(h * BANK, (h + 1) * BANK)
+            nc.vector.quantize_mx(
+                out=z2_codes[:, cols].bitcast(FP8X4),
+                scales=z2_plane[:, cols],
+                in_=z2_grouped[h][:].rearrange("p c t -> p (c t)"),
+            )
+        for m in range(1, PACK):
+            interleave_z(m)
+        for m in range(1, PACK):
+            quantize_z(m)
+
+        out_rows = out.rearrange("(p m) w -> m p w", m=PACK)
+        halves = [slice(h * BANK, (h + 1) * BANK) for h in range(2)]
+        n3_halves = [n3_list[:, h * (BANK // 16) : (h + 1) * (BANK // 16)] for h in range(2)]
+        mixed = {}
+        s_rows = {}
+
+        def first_step(m):
+            half_s = ring.tile([P, U], F32, name="half_s")
+            minus_s = ring.tile([P, U], F32, name="minus_s")
+            s_rows[m] = ring.tile([P, U], F32, name="s_rows")
+            banks = []
+            for h in range(2):
+                s_bank = psum.tile([P, BANK], F32, name="s_bank", tag="second%d" % ((2 * m + h) % 4))
+                product(s_bank, z_codes, z_plane, m, z2_codes[:, halves[h]], z2_plane[:, halves[h]])
+                nc.scalar.activation(half_s[:, halves[h]], s_bank[:], ACT.Copy, scale=0.5 * 0.0625)
+                banks.append(s_bank)
+            for h in range(2):
+                if m == 0:
+                    nc.vector.tensor_scalar(minus_s[:, halves[1 - h]], banks[1 - h][:], -1.5 * 0.0625, None, ALU.mult)
+                else:
+                    nc.scalar.activation(minus_s[:, halves[h]], banks[h][:], ACT.Copy, scale=-1.5 * 0.0625)
+            for h in range(2):
+                nc.scalar.activation(s_rows[m][:, halves[h]], banks[h][:], ACT.Copy, scale=0.0625)
+            mixed[m] = ring.tile([P, U], F32, name="mixed")
+            for h in range(2):
+                nc.vector.tensor_tensor(
+                    mixed[m][:, halves[h]], half_s[:].indirect(n3_halves[h]), minus_s[:, halves[h]], ALU.add
+                )
+
+        def second_step(m):
+            result = ring.tile([P, U], F32, name="result")
+            for h in range(2):
+                nc.vector.tensor_tensor(
+                    result[:, halves[h]], mixed[m][:].indirect(n3_halves[h]), s_rows[m][:, halves[h]], ALU.add
+                )
+                nc.sync.dma_start(out_rows[m][:, halves[h]], result[:, halves[h]])
+
+        for m in range(PACK):
+            first_step(m)
+            second_step(m)

@@ -18,6 +18,7 @@ ALU = mybir.AluOpType
 P = 128
 PACK = 4
 BANK = 512
+RUN = 8
 
 
 def tile_picked_ckqnormpagetwice_none_p_kernel(
@@ -33,6 +34,20 @@ def tile_picked_ckqnormpagetwice_none_p_kernel(
             tile = keep.tile(list(src.shape), U16, name=name)
             nc.sync.dma_start(tile[:], src)
             return tile
+
+        def load_columns(src, name):
+            rows = src.rearrange("(b t r) o -> t b r o", t=PACK, r=RUN)
+            columns = []
+            for t in range(PACK):
+                column = keep.tile([P, 1], F32, name="%s_col%d" % (name, t))
+                nc.sync.dma_start(column[:], rows[t])
+                columns.append(column)
+            return columns
+
+        ones = keep.tile([P, 1], F32)
+        warm = keep.tile([P, 1], F32)
+        nc.vector.memset(ones[:], 1.0)
+        nc.scalar.activation(warm[:], ones[:], ACT.Ln)
 
         k1_list = load_list(k1, "k1_list")
         d_scale_table = keep.tile([P, G], U8, align_bytes=64)
@@ -54,17 +69,16 @@ def tile_picked_ckqnormpagetwice_none_p_kernel(
         d_word_table = keep.tile([P, G], U32, align_bytes=64)
         nc.sync.dma_start(d_word_table[:].bitcast(I32), d_words[0].rearrange("p n t -> p (n t)").bitcast(I32))
         n2_list = load_list(n2, "n2_list")
-        mem_rows = mem.rearrange("(p t) w -> t p w", t=PACK)
+        mem_rows = mem.rearrange("(b t r) w -> t b r w", t=PACK, r=RUN)
         pages = []
         for t in range(PACK):
             page = keep.tile([P, U], F32, name="page%d" % t)
             nc.sync.dma_start(page[:], mem_rows[t])
             pages.append(page)
         n1_list = load_list(n1, "n1_list")
-        ga_cols = keep.tile([P, PACK], F32)
-        gb_cols = keep.tile([P, PACK], F32)
-        nc.sync.dma_start(ga_cols[:], ga.rearrange("(p t) o -> p (t o)", t=PACK))
-        nc.sync.dma_start(gb_cols[:], gb.rearrange("(p t) o -> p (t o)", t=PACK))
+        with nc.allow_non_contiguous_dma(reason="one weight for each partition and row tile"):
+            gb_cols = load_columns(gb, "gb")
+            ga_cols = load_columns(ga, "ga")
         n3_list = load_list(n3, "n3_list")
 
         def gather(table, offsets, dtype, name):
@@ -75,8 +89,8 @@ def tile_picked_ckqnormpagetwice_none_p_kernel(
         d_scales_picked = gather(d_scale_table, k1_list, U8, "d_scales_picked")
         d_scales_dealt = keep.tile([P, H], U8, align_bytes=64)
         nc.vector.tensor_copy(
-            d_scales_dealt[:].rearrange("p (t m) -> p m t", t=PACK),
-            d_scales_picked[:].rearrange("p (m t) -> p m t", t=PACK),
+            d_scales_dealt[:].bitcast(I32).rearrange("p (t b r) -> p b t r", t=PACK, r=RUN // 4),
+            d_scales_picked[:].bitcast(I32).rearrange("p (b t r) -> p b t r", t=PACK, r=RUN // 4),
         )
         d_plane = keep.tile([P, H], U8, align_bytes=64)
         nc.vector.tensor_copy(d_plane[:].bitcast(I32), d_scales_dealt[:].bitcast(I32))
@@ -89,8 +103,8 @@ def tile_picked_ckqnormpagetwice_none_p_kernel(
 
         w_grouped = keep.tile([P, PACK * H], BF16, align_bytes=64)
         nc.scalar.copy(
-            w_grouped[:].rearrange("p (t m j) -> p m t j", t=PACK, j=PACK),
-            w_raw[:].rearrange("p j (m t) -> p m t j", t=PACK),
+            w_grouped[:].rearrange("p (t b r j) -> p b t r j", t=PACK, r=RUN, j=PACK),
+            w_raw[:].rearrange("p j (b t r) -> p b t r j", t=PACK, r=RUN),
         )
         w_codes = keep.tile([P, H], U32, align_bytes=64)
         w_plane = keep.tile([P, H], U8, align_bytes=64)
@@ -99,8 +113,8 @@ def tile_picked_ckqnormpagetwice_none_p_kernel(
         d_words_picked = gather(d_word_table, k1_list, U32, "d_words_picked")
         d_codes = keep.tile([P, H], U32, align_bytes=64)
         nc.vector.tensor_copy(
-            d_codes[:].rearrange("p (t m) -> p m t", t=PACK),
-            d_words_picked[:].rearrange("p (m t) -> p m t", t=PACK),
+            d_codes[:].rearrange("p (t b r) -> p b t r", t=PACK, r=RUN),
+            d_words_picked[:].rearrange("p (b t r) -> p b t r", t=PACK, r=RUN),
         )
 
         def product(bank, codes, plane, t, moving_codes, moving_plane):
@@ -128,7 +142,7 @@ def tile_picked_ckqnormpagetwice_none_p_kernel(
         for t in range(PACK):
             a_bank = psum.tile([P, BANK], F32, name="a_bank%d" % t, tag="first%d" % t)
             product(a_bank, d_codes, d_plane, t, offs_words[:], offs_scales[:])
-            log_tile = keep.tile([P, 2 * S], F32, name="log_tile%d" % t, tag="shared%d" % t, align_bytes=64)
+            log_tile = keep.tile([P, 2 * S], F32, name="log_tile%d" % t, align_bytes=64)
             nc.scalar.activation(log_tile[:, S:], a_bank[:], ACT.Abs)
             a_banks.append(a_bank)
             logs.append(log_tile)
@@ -140,77 +154,62 @@ def tile_picked_ckqnormpagetwice_none_p_kernel(
         z_planes = keep.tile([P, PACK, S], BF16, align_bytes=64)
         for t in range(PACK):
             nc.vector.scalar_tensor_tensor(
-                z_planes[:, t, :], a_banks[t][:], ga_cols[:, t : t + 1], inverse[:, t, :], ALU.mult, ALU.mult
+                z_planes[:, t, :], a_banks[t][:], ga_cols[t][:], inverse[:, t, :], ALU.mult, ALU.mult
             )
 
-        z_grouped = keep.tile([P, PACK, P, PACK], BF16, align_bytes=64)
+        halves = [slice(h * BANK, (h + 1) * BANK) for h in range(2)]
+        z2_grouped = [keep.tile([P, BANK, PACK], BF16, name="z2_grouped%d" % h, align_bytes=64) for h in range(2)]
+        for t in range(PACK):
+            for h in range(2):
+                if t >= 2 and h == 0:
+                    nc.scalar.activation(
+                        z2_grouped[h][:, :, t], pages[t][:, halves[h]], ACT.Copy, scale=gb_cols[t][:]
+                    )
+                else:
+                    nc.gpsimd.tensor_scalar(
+                        z2_grouped[h][:, :, t], pages[t][:, halves[h]], gb_cols[t][:], 0.0, ALU.mult, ALU.add
+                    )
+
+        z_grouped = keep.tile([P, PACK, P * PACK], BF16, align_bytes=64)
         z_codes = keep.tile([P, S], U32, align_bytes=64)
         z_plane = keep.tile([P, S], U8, align_bytes=64)
-        z_dealt = z_planes[:].rearrange("p t (c m) -> p m c t", m=PACK)
+        z_dealt = z_planes[:].rearrange("p t (b m r) -> p m b r t", m=PACK, r=RUN)
 
-        def interleave_z(m):
-            nc.vector.tensor_copy(z_grouped[:, m], z_dealt[:, m])
-
-        def quantize_z(m):
+        def quantize_z(m, copy):
             cols = slice(m * P, (m + 1) * P)
-            nc.vector.quantize_mx(
-                out=z_codes[:, cols].bitcast(FP8X4),
-                scales=z_plane[:, cols],
-                in_=z_grouped[:, m].rearrange("p c t -> p (c t)"),
-            )
+            copy(z_grouped[:, m, :].rearrange("p (b r t) -> p b r t", r=RUN, t=PACK), z_dealt[:, m])
+            nc.vector.quantize_mx(out=z_codes[:, cols].bitcast(FP8X4), scales=z_plane[:, cols], in_=z_grouped[:, m, :])
 
         z2_codes = keep.tile([P, U], U32, align_bytes=64)
         z2_plane = keep.tile([P, U], U8, align_bytes=64)
-        z2_grouped = []
-        interleave_z(0)
+        quantize_z(0, nc.vector.tensor_copy)
         for h in range(2):
-            z2_planes = keep.tile([P, PACK, BANK], BF16, name="z2_planes%d" % h, tag="shared%d" % (3 - h), align_bytes=64)
-            for t in range(PACK):
-                nc.scalar.activation(
-                    z2_planes[:, t, :], pages[t][:, h * BANK : (h + 1) * BANK], ACT.Copy, scale=gb_cols[:, t : t + 1]
-                )
-            grouped = keep.tile([P, BANK, PACK], BF16, name="z2_grouped%d" % h, align_bytes=64)
-            nc.vector.tensor_copy(
-                grouped[:].rearrange("p (c i) t -> p c t i", i=4),
-                z2_planes[:].rearrange("p t (c i) -> p c t i", i=4),
-            )
-            z2_grouped.append(grouped)
-        quantize_z(0)
-        for h in range(2):
-            cols = slice(h * BANK, (h + 1) * BANK)
             nc.vector.quantize_mx(
-                out=z2_codes[:, cols].bitcast(FP8X4),
-                scales=z2_plane[:, cols],
+                out=z2_codes[:, halves[h]].bitcast(FP8X4),
+                scales=z2_plane[:, halves[h]],
                 in_=z2_grouped[h][:].rearrange("p c t -> p (c t)"),
             )
         for m in range(1, PACK):
-            interleave_z(m)
-        for m in range(1, PACK):
-            quantize_z(m)
+            quantize_z(m, nc.scalar.copy)
 
-        out_rows = out.rearrange("(p m) w -> m p w", m=PACK)
-        halves = [slice(h * BANK, (h + 1) * BANK) for h in range(2)]
+        out_rows = out.rearrange("(b m r) w -> m b r w", m=PACK, r=RUN)
         n3_halves = [n3_list[:, h * (BANK // 16) : (h + 1) * (BANK // 16)] for h in range(2)]
+        s_banks = {}
         mixed = {}
-        s_rows = {}
 
         def first_step(m):
             half_s = ring.tile([P, U], F32, name="half_s")
             minus_s = ring.tile([P, U], F32, name="minus_s")
-            s_rows[m] = ring.tile([P, U], F32, name="s_rows")
-            banks = []
             for h in range(2):
-                s_bank = psum.tile([P, BANK], F32, name="s_bank", tag="second%d" % ((2 * m + h) % 4))
-                product(s_bank, z_codes, z_plane, m, z2_codes[:, halves[h]], z2_plane[:, halves[h]])
-                nc.scalar.activation(half_s[:, halves[h]], s_bank[:], ACT.Copy, scale=0.5 * 0.0625)
-                banks.append(s_bank)
+                tag = ("second%d" if m < 2 else "first%d") % ((2 * m + h) % 4)
+                s_banks[m, h] = psum.tile([P, BANK], F32, name="s_bank", tag=tag)
+                product(s_banks[m, h], z_codes, z_plane, m, z2_codes[:, halves[h]], z2_plane[:, halves[h]])
+                nc.scalar.activation(half_s[:, halves[h]], s_banks[m, h][:], ACT.Copy, scale=0.5 * 0.0625)
             for h in range(2):
                 if m == 0:
-                    nc.vector.tensor_scalar(minus_s[:, halves[1 - h]], banks[1 - h][:], -1.5 * 0.0625, None, ALU.mult)
+                    nc.vector.tensor_scalar(minus_s[:, halves[1 - h]], s_banks[m, 1 - h][:], -1.5 * 0.0625, None, ALU.mult)
                 else:
-                    nc.scalar.activation(minus_s[:, halves[h]], banks[h][:], ACT.Copy, scale=-1.5 * 0.0625)
-            for h in range(2):
-                nc.scalar.activation(s_rows[m][:, halves[h]], banks[h][:], ACT.Copy, scale=0.0625)
+                    nc.scalar.activation(minus_s[:, halves[h]], s_banks[m, h][:], ACT.Copy, scale=-1.5 * 0.0625)
             mixed[m] = ring.tile([P, U], F32, name="mixed")
             for h in range(2):
                 nc.vector.tensor_tensor(
@@ -218,13 +217,17 @@ def tile_picked_ckqnormpagetwice_none_p_kernel(
                 )
 
         def second_step(m):
+            s_rows = ring.tile([P, U], F32, name="s_rows")
             result = ring.tile([P, U], F32, name="result")
             for h in range(2):
+                nc.scalar.activation(s_rows[:, halves[h]], s_banks[m, h][:], ACT.Copy, scale=0.0625)
                 nc.vector.tensor_tensor(
-                    result[:, halves[h]], mixed[m][:].indirect(n3_halves[h]), s_rows[m][:, halves[h]], ALU.add
+                    result[:, halves[h]], mixed[m][:].indirect(n3_halves[h]), s_rows[:, halves[h]], ALU.add
                 )
-                nc.sync.dma_start(out_rows[m][:, halves[h]], result[:, halves[h]])
+                nc.sync.dma_start(out_rows[m][:, :, halves[h]], result[:, halves[h]])
 
-        for m in range(PACK):
+        first_step(0)
+        for m in range(1, PACK):
             first_step(m)
-            second_step(m)
+            second_step(m - 1)
+        second_step(PACK - 1)

@@ -40,7 +40,8 @@ def tile_picked_ckqnormpagetwice_none_p_kernel(
             columns = []
             for t in range(PACK):
                 column = keep.tile([P, 1], F32, name="%s_col%d" % (name, t))
-                nc.sync.dma_start(column[:], rows[t])
+                with nc.allow_non_contiguous_dma(reason="one weight for each partition"):
+                    nc.gpsimd.dma_start(column[:], rows[t])
                 columns.append(column)
             return columns
 
@@ -55,17 +56,22 @@ def tile_picked_ckqnormpagetwice_none_p_kernel(
             d_scale_table[:].bitcast(I32), d_scales[0].bitcast(I32).unsqueeze(1).to_broadcast([16, 8, G // 4])
         )
         two_list = load_list(two, "two_list")
-        offs_list = load_list(offs, "offs_list")
         x_word_table = keep.tile([P, T], U32, align_bytes=64)
         nc.sync.dma_start(x_word_table[:].bitcast(I32), x_words[0].rearrange("p n t -> p (n t)").bitcast(I32))
-        w_raw = keep.tile([P, PACK, H], F32)
-        nc.sync.dma_start(w_raw[:], w1.rearrange("(p j) c -> p j c", j=PACK))
         x_scale_table = keep.tile([P, T], U8, align_bytes=64)
         for q in range(4):
             nc.sync.dma_start(
                 x_scale_table[32 * q : 32 * q + 32, :].bitcast(I32),
                 x_scales[0, 4 * q : 4 * q + 4, :].bitcast(I32).unsqueeze(0).to_broadcast([8, 4, T // 4]),
             )
+        w_rows = w1.rearrange("(p j) c -> p j c", j=PACK)
+        w_raw = []
+        for u in range(2):
+            w_half = keep.tile([P, PACK, H // 2], F32, name="w_half%d" % u)
+            nc.sync.dma_start(w_half[:], w_rows[:, :, u * (H // 2) : (u + 1) * (H // 2)])
+            w_raw.append(w_half)
+            if u == 0:
+                offs_list = load_list(offs, "offs_list")
         d_word_table = keep.tile([P, G], U32, align_bytes=64)
         nc.sync.dma_start(d_word_table[:].bitcast(I32), d_words[0].rearrange("p n t -> p (n t)").bitcast(I32))
         n2_list = load_list(n2, "n2_list")
@@ -75,14 +81,13 @@ def tile_picked_ckqnormpagetwice_none_p_kernel(
             page = keep.tile([P, U], F32, name="page%d" % t)
             nc.sync.dma_start(page[:], mem_rows[t])
             pages.append(page)
+        gb_cols = load_columns(gb, "gb")
         n1_list = load_list(n1, "n1_list")
-        with nc.allow_non_contiguous_dma(reason="one weight for each partition and row tile"):
-            gb_cols = load_columns(gb, "gb")
-            ga_cols = load_columns(ga, "ga")
+        ga_cols = load_columns(ga, "ga")
         n3_list = load_list(n3, "n3_list")
 
-        def gather(table, offsets, dtype, name):
-            picked = keep.tile([P, S], dtype, name=name, align_bytes=64)
+        def gather(table, offsets, dtype, name, tag=None):
+            picked = keep.tile([P, S], dtype, name=name, tag=tag or name, align_bytes=64)
             nc.vector.tensor_copy(picked[:], table[:].indirect(offsets[:]))
             return picked
 
@@ -97,19 +102,18 @@ def tile_picked_ckqnormpagetwice_none_p_kernel(
         for r in range(1, 4):
             nc.scalar.dma_start(d_plane[r:P:32, :].bitcast(I32), d_scales_dealt[8 * r : P : 32, :].bitcast(I32))
         two_words = gather(x_word_table, two_list, U32, "two_words")
-        offs_words = gather(x_word_table, offs_list, U32, "offs_words")
         two_scales = gather(x_scale_table, two_list, U8, "two_scales")
-        offs_scales = gather(x_scale_table, offs_list, U8, "offs_scales")
+        offs_words = gather(x_word_table, offs_list, U32, "offs_words")
 
-        w_grouped = keep.tile([P, PACK * H], BF16, align_bytes=64)
-        nc.scalar.copy(
-            w_grouped[:].rearrange("p (t b r j) -> p b t r j", t=PACK, r=RUN, j=PACK),
-            w_raw[:].rearrange("p j (b t r) -> p b t r j", t=PACK, r=RUN),
-        )
+        w_grouped = keep.tile([P, PACK * H], BF16, tag="w_grouped", align_bytes=64)
+        w_dealt = w_grouped[:].rearrange("p (t u b r j) -> p u b t r j", t=PACK, u=2, r=RUN, j=PACK)
+        for u in range(2):
+            nc.scalar.copy(w_dealt[:, u], w_raw[u][:].rearrange("p j (b t r) -> p b t r j", t=PACK, r=RUN))
         w_codes = keep.tile([P, H], U32, align_bytes=64)
         w_plane = keep.tile([P, H], U8, align_bytes=64)
         nc.vector.quantize_mx(out=w_codes[:].bitcast(FP8X4), scales=w_plane[:], in_=w_grouped[:])
 
+        offs_scales = gather(x_scale_table, offs_list, U8, "offs_scales", tag="w_grouped")
         d_words_picked = gather(d_word_table, k1_list, U32, "d_words_picked")
         d_codes = keep.tile([P, H], U32, align_bytes=64)
         nc.vector.tensor_copy(
@@ -131,7 +135,7 @@ def tile_picked_ckqnormpagetwice_none_p_kernel(
 
         b_rows = keep.tile([P, PACK, V], F32)
         for t in range(PACK):
-            b_bank = psum.tile([P, BANK], F32, name="b_bank%d" % t, tag="second%d" % t)
+            b_bank = psum.tile([P, BANK], F32, name="b_bank%d" % t, tag="first%d" % t)
             product(b_bank, w_codes, w_plane, t, two_words[:], two_scales[:])
             nc.scalar.copy(b_rows[:, t, :], b_bank[:])
         for t in range(PACK):
@@ -142,13 +146,13 @@ def tile_picked_ckqnormpagetwice_none_p_kernel(
         for t in range(PACK):
             a_bank = psum.tile([P, BANK], F32, name="a_bank%d" % t, tag="first%d" % t)
             product(a_bank, d_codes, d_plane, t, offs_words[:], offs_scales[:])
-            log_tile = keep.tile([P, 2 * S], F32, name="log_tile%d" % t, align_bytes=64)
+            log_tile = keep.tile([P, 2 * S], F32, name="log_tile%d" % t, tag="log%d" % t, align_bytes=64)
             nc.scalar.activation(log_tile[:, S:], a_bank[:], ACT.Abs)
             a_banks.append(a_bank)
             logs.append(log_tile)
         for t in range(PACK):
             nc.scalar.activation(logs[t][:, :S], logs[t][:, S:], ACT.Ln, bias=8.0)
-        inverse = keep.tile([P, PACK, S], F32)
+        inverse = keep.tile([P, PACK, S], F32, tag="inverse", align_bytes=64)
         for t in range(PACK):
             nc.scalar.activation(inverse[:, t, :], logs[t][:].indirect(n1_list[:]), ACT.Exp, scale=-1.0)
         z_planes = keep.tile([P, PACK, S], BF16, align_bytes=64)
@@ -158,17 +162,18 @@ def tile_picked_ckqnormpagetwice_none_p_kernel(
             )
 
         halves = [slice(h * BANK, (h + 1) * BANK) for h in range(2)]
-        z2_grouped = [keep.tile([P, BANK, PACK], BF16, name="z2_grouped%d" % h, align_bytes=64) for h in range(2)]
+        pieces = [slice(0, 512), slice(512, 768), slice(768, 1024)]
+        z2_grouped = [
+            keep.tile([P, 512, PACK], BF16, name="z2_grouped0", align_bytes=64),
+            keep.tile([P, 256, PACK], BF16, name="z2_grouped1", align_bytes=64),
+            keep.tile([P, 256, PACK], BF16, name="z2_grouped2", tag="log3", align_bytes=64),
+        ]
         for t in range(PACK):
-            for h in range(2):
-                if t >= 2 and h == 0:
-                    nc.scalar.activation(
-                        z2_grouped[h][:, :, t], pages[t][:, halves[h]], ACT.Copy, scale=gb_cols[t][:]
-                    )
-                else:
-                    nc.gpsimd.tensor_scalar(
-                        z2_grouped[h][:, :, t], pages[t][:, halves[h]], gb_cols[t][:], 0.0, ALU.mult, ALU.add
-                    )
+            nc.scalar.activation(z2_grouped[2][:, :, t], pages[t][:, pieces[2]], ACT.Copy, scale=gb_cols[t][:])
+            for i in (0, 1):
+                nc.gpsimd.tensor_scalar(
+                    z2_grouped[i][:, :, t], pages[t][:, pieces[i]], gb_cols[t][:], 0.0, ALU.mult, ALU.add
+                )
 
         z_grouped = keep.tile([P, PACK, P * PACK], BF16, align_bytes=64)
         z_codes = keep.tile([P, S], U32, align_bytes=64)
@@ -180,14 +185,14 @@ def tile_picked_ckqnormpagetwice_none_p_kernel(
             copy(z_grouped[:, m, :].rearrange("p (b r t) -> p b r t", r=RUN, t=PACK), z_dealt[:, m])
             nc.vector.quantize_mx(out=z_codes[:, cols].bitcast(FP8X4), scales=z_plane[:, cols], in_=z_grouped[:, m, :])
 
-        z2_codes = keep.tile([P, U], U32, align_bytes=64)
+        z2_codes = keep.tile([P, U], U32, tag="inverse", align_bytes=64)
         z2_plane = keep.tile([P, U], U8, align_bytes=64)
         quantize_z(0, nc.vector.tensor_copy)
-        for h in range(2):
+        for i in range(3):
             nc.vector.quantize_mx(
-                out=z2_codes[:, halves[h]].bitcast(FP8X4),
-                scales=z2_plane[:, halves[h]],
-                in_=z2_grouped[h][:].rearrange("p c t -> p (c t)"),
+                out=z2_codes[:, pieces[i]].bitcast(FP8X4),
+                scales=z2_plane[:, pieces[i]],
+                in_=z2_grouped[i][:].rearrange("p c t -> p (c t)"),
             )
         for m in range(1, PACK):
             quantize_z(m, nc.scalar.copy)
@@ -206,8 +211,8 @@ def tile_picked_ckqnormpagetwice_none_p_kernel(
                 product(s_banks[m, h], z_codes, z_plane, m, z2_codes[:, halves[h]], z2_plane[:, halves[h]])
                 nc.scalar.activation(half_s[:, halves[h]], s_banks[m, h][:], ACT.Copy, scale=0.5 * 0.0625)
             for h in range(2):
-                if m == 0:
-                    nc.vector.tensor_scalar(minus_s[:, halves[1 - h]], s_banks[m, 1 - h][:], -1.5 * 0.0625, None, ALU.mult)
+                if m == 0 and h == 0:
+                    nc.vector.tensor_scalar(minus_s[:, halves[h]], s_banks[m, h][:], -1.5 * 0.0625, None, ALU.mult)
                 else:
                     nc.scalar.activation(minus_s[:, halves[h]], s_banks[m, h][:], ACT.Copy, scale=-1.5 * 0.0625)
             mixed[m] = ring.tile([P, U], F32, name="mixed")
@@ -221,10 +226,12 @@ def tile_picked_ckqnormpagetwice_none_p_kernel(
             result = ring.tile([P, U], F32, name="result")
             for h in range(2):
                 nc.scalar.activation(s_rows[:, halves[h]], s_banks[m, h][:], ACT.Copy, scale=0.0625)
-                nc.vector.tensor_tensor(
-                    result[:, halves[h]], mixed[m][:].indirect(n3_halves[h]), s_rows[:, halves[h]], ALU.add
-                )
-                nc.sync.dma_start(out_rows[m][:, :, halves[h]], result[:, halves[h]])
+                width = BANK // 2 if (m, h) == (PACK - 1, 1) else BANK
+                for c in range(h * BANK, (h + 1) * BANK, width):
+                    cols = slice(c, c + width)
+                    offsets = n3_list[:, c // 16 : (c + width) // 16]
+                    nc.vector.tensor_tensor(result[:, cols], mixed[m][:].indirect(offsets), s_rows[:, cols], ALU.add)
+                    nc.sync.dma_start(out_rows[m][:, :, cols], result[:, cols])
 
         first_step(0)
         for m in range(1, PACK):

@@ -1,6 +1,7 @@
 from contextlib import ExitStack
 
 import concourse.mybir as mybir
+from concourse.masks import make_identity
 
 K, T, S, V, G, H, U = 512, 1024, 512, 512, 2048, 512, 1024
 FLOPS = 2 * K * H * S + 2 * K * H * V + 2 * H * S * U
@@ -34,16 +35,6 @@ def tile_picked_ckqnormpagetwice_none_p_kernel(
             tile = keep.tile(list(src.shape), U16, name=name)
             nc.sync.dma_start(tile[:], src)
             return tile
-
-        def load_columns(src, name):
-            rows = src.rearrange("(b t r) o -> t b r o", t=PACK, r=RUN)
-            columns = []
-            for t in range(PACK):
-                column = keep.tile([P, 1], F32, name="%s_col%d" % (name, t))
-                with nc.allow_non_contiguous_dma(reason="one weight for each partition"):
-                    nc.gpsimd.dma_start(column[:], rows[t])
-                columns.append(column)
-            return columns
 
         ones = keep.tile([P, 1], F32)
         warm = keep.tile([P, 1], F32)
@@ -81,10 +72,23 @@ def tile_picked_ckqnormpagetwice_none_p_kernel(
             page = keep.tile([P, U], F32, name="page%d" % t)
             nc.sync.dma_start(page[:], mem_rows[t])
             pages.append(page)
-        gb_cols = load_columns(gb, "gb")
         n1_list = load_list(n1, "n1_list")
-        ga_cols = load_columns(ga, "ga")
         n3_list = load_list(n3, "n3_list")
+
+        identity = keep.tile([P, P], F32)
+        make_identity(nc, identity[:])
+        weight_rows = keep.tile([P, P], F32)
+        nc.gpsimd.memset(weight_rows[:], 0.0)
+        for row, src in ((0, ga), (PACK, gb)):
+            nc.gpsimd.dma_start(
+                weight_rows[row : row + PACK, :], src.rearrange("(b t r) o -> t b (r o)", t=PACK, r=RUN)
+            )
+        weight_bank = psum.tile([P, P], F32, tag="second0")
+        nc.tensor.transpose(weight_bank[:], weight_rows[:], identity[:])
+        weight_cols = keep.tile([P, 2 * PACK], F32)
+        nc.scalar.copy(weight_cols[:], weight_bank[:, : 2 * PACK])
+        ga_cols = [weight_cols[:, t : t + 1] for t in range(PACK)]
+        gb_cols = [weight_cols[:, PACK + t : PACK + t + 1] for t in range(PACK)]
 
         def gather(table, offsets, dtype, name, tag=None):
             picked = keep.tile([P, S], dtype, name=name, tag=tag or name, align_bytes=64)
@@ -104,6 +108,7 @@ def tile_picked_ckqnormpagetwice_none_p_kernel(
         two_words = gather(x_word_table, two_list, U32, "two_words")
         two_scales = gather(x_scale_table, two_list, U8, "two_scales")
         offs_words = gather(x_word_table, offs_list, U32, "offs_words")
+        offs_scales = gather(x_scale_table, offs_list, U8, "offs_scales")
 
         w_grouped = keep.tile([P, PACK * H], BF16, tag="w_grouped", align_bytes=64)
         w_dealt = w_grouped[:].rearrange("p (t u b r j) -> p u b t r j", t=PACK, u=2, r=RUN, j=PACK)
@@ -113,8 +118,7 @@ def tile_picked_ckqnormpagetwice_none_p_kernel(
         w_plane = keep.tile([P, H], U8, align_bytes=64)
         nc.vector.quantize_mx(out=w_codes[:].bitcast(FP8X4), scales=w_plane[:], in_=w_grouped[:])
 
-        offs_scales = gather(x_scale_table, offs_list, U8, "offs_scales", tag="w_grouped")
-        d_words_picked = gather(d_word_table, k1_list, U32, "d_words_picked")
+        d_words_picked = gather(d_word_table, k1_list, U32, "d_words_picked", tag="w_grouped")
         d_codes = keep.tile([P, H], U32, align_bytes=64)
         nc.vector.tensor_copy(
             d_codes[:].rearrange("p (t b r) -> p b t r", t=PACK, r=RUN),
@@ -158,44 +162,45 @@ def tile_picked_ckqnormpagetwice_none_p_kernel(
         z_planes = keep.tile([P, PACK, S], BF16, align_bytes=64)
         for t in range(PACK):
             nc.vector.scalar_tensor_tensor(
-                z_planes[:, t, :], a_banks[t][:], ga_cols[t][:], inverse[:, t, :], ALU.mult, ALU.mult
+                z_planes[:, t, :], a_banks[t][:], ga_cols[t], inverse[:, t, :], ALU.mult, ALU.mult
             )
 
         halves = [slice(h * BANK, (h + 1) * BANK) for h in range(2)]
-        pieces = [slice(0, 512), slice(512, 768), slice(768, 1024)]
-        z2_grouped = [
-            keep.tile([P, 512, PACK], BF16, name="z2_grouped0", align_bytes=64),
-            keep.tile([P, 256, PACK], BF16, name="z2_grouped1", align_bytes=64),
-            keep.tile([P, 256, PACK], BF16, name="z2_grouped2", tag="log3", align_bytes=64),
-        ]
+        late_cols = keep.tile([P, 2 * PACK], F32, tag="log3", align_bytes=64)
+        nc.scalar.copy(late_cols[:], weight_bank[:, : 2 * PACK])
+        z2_grouped = [keep.tile([P, BANK, PACK], BF16, name="z2_grouped", tag="z2_grouped%d" % h, align_bytes=64) for h in range(2)]
         for t in range(PACK):
-            nc.scalar.activation(z2_grouped[2][:, :, t], pages[t][:, pieces[2]], ACT.Copy, scale=gb_cols[t][:])
-            for i in (0, 1):
-                nc.gpsimd.tensor_scalar(
-                    z2_grouped[i][:, :, t], pages[t][:, pieces[i]], gb_cols[t][:], 0.0, ALU.mult, ALU.add
-                )
+            for h in range(2):
+                if t >= 2 and h == 1:
+                    nc.scalar.activation(
+                        z2_grouped[h][:, :, t], pages[t][:, halves[h]], ACT.Copy, scale=late_cols[:, PACK + t : PACK + t + 1]
+                    )
+                else:
+                    nc.gpsimd.tensor_scalar(
+                        z2_grouped[h][:, :, t], pages[t][:, halves[h]], gb_cols[t], 0.0, ALU.mult, ALU.add
+                    )
 
-        z_grouped = keep.tile([P, PACK, P * PACK], BF16, align_bytes=64)
         z_codes = keep.tile([P, S], U32, align_bytes=64)
         z_plane = keep.tile([P, S], U8, align_bytes=64)
         z_dealt = z_planes[:].rearrange("p t (b m r) -> p m b r t", m=PACK, r=RUN)
 
         def quantize_z(m, copy):
             cols = slice(m * P, (m + 1) * P)
-            copy(z_grouped[:, m, :].rearrange("p (b r t) -> p b r t", r=RUN, t=PACK), z_dealt[:, m])
-            nc.vector.quantize_mx(out=z_codes[:, cols].bitcast(FP8X4), scales=z_plane[:, cols], in_=z_grouped[:, m, :])
+            tag = "z_grouped%d" % m if m < 2 else "z2_grouped%d" % (m - 2)
+            z_grouped = keep.tile([P, P * PACK], BF16, name="z_grouped", tag=tag, align_bytes=64)
+            copy(z_grouped[:].rearrange("p (b r t) -> p b r t", r=RUN, t=PACK), z_dealt[:, m])
+            nc.vector.quantize_mx(out=z_codes[:, cols].bitcast(FP8X4), scales=z_plane[:, cols], in_=z_grouped[:])
 
         z2_codes = keep.tile([P, U], U32, tag="inverse", align_bytes=64)
         z2_plane = keep.tile([P, U], U8, align_bytes=64)
         quantize_z(0, nc.vector.tensor_copy)
-        for i in range(3):
+        for h in range(2):
             nc.vector.quantize_mx(
-                out=z2_codes[:, pieces[i]].bitcast(FP8X4),
-                scales=z2_plane[:, pieces[i]],
-                in_=z2_grouped[i][:].rearrange("p c t -> p (c t)"),
+                out=z2_codes[:, halves[h]].bitcast(FP8X4),
+                scales=z2_plane[:, halves[h]],
+                in_=z2_grouped[h][:].rearrange("p c t -> p (c t)"),
             )
-        for m in range(1, PACK):
-            quantize_z(m, nc.scalar.copy)
+        quantize_z(1, nc.scalar.copy)
 
         out_rows = out.rearrange("(b m r) w -> m b r w", m=PACK, r=RUN)
         n3_halves = [n3_list[:, h * (BANK // 16) : (h + 1) * (BANK // 16)] for h in range(2)]
@@ -236,5 +241,8 @@ def tile_picked_ckqnormpagetwice_none_p_kernel(
         first_step(0)
         for m in range(1, PACK):
             first_step(m)
+            if m == 1:
+                quantize_z(2, nc.scalar.copy)
+                quantize_z(3, nc.scalar.copy)
             second_step(m - 1)
         second_step(PACK - 1)

from contextlib import ExitStack

import concourse.mybir as mybir
from concourse.masks import make_identity

K, T, S, V, G, H, U = 512, 1024, 512, 512, 2048, 512, 1024
FLOPS = 2 * K * H * S + 2 * K * H * V + 2 * H * S * U

F32 = mybir.dt.float32
BF16 = mybir.dt.bfloat16
I32 = mybir.dt.int32
U32 = mybir.dt.uint32
U16 = mybir.dt.uint16
U8 = mybir.dt.uint8
FP8X4 = mybir.dt.float8_e4m3fn_x4
ACT = mybir.ActivationFunctionType
ALU = mybir.AluOpType

P = 128
PACK = 4
BANK = 512
RUN = 8


def tile_picked_ckqnormpagetwice_none_p_kernel(
    tc, x_words, x_scales, d_words, d_scales, w1, mem, ga, gb, offs, k1, two, n1, n2, n3, out
):
    nc = tc.nc
    with ExitStack() as ctx:
        keep = ctx.enter_context(tc.tile_pool(name="keep", bufs=1))
        ring = ctx.enter_context(tc.tile_pool(name="ring", bufs=3))
        psum = ctx.enter_context(tc.psum_pool(name="psum", bufs=1))

        def load_list(src, name):
            tile = keep.tile(list(src.shape), U16, name=name)
            nc.sync.dma_start(tile[:], src)
            return tile

        ones = keep.tile([P, 1], F32)
        warm = keep.tile([P, 1], F32)
        nc.vector.memset(ones[:], 1.0)
        nc.scalar.activation(warm[:], ones[:], ACT.Ln)

        k1_list = load_list(k1, "k1_list")
        d_scale_table = keep.tile([P, G], U8, align_bytes=64)
        nc.sync.dma_start(
            d_scale_table[:].bitcast(I32), d_scales[0].bitcast(I32).unsqueeze(1).to_broadcast([16, 8, G // 4])
        )
        two_list = load_list(two, "two_list")
        x_word_table = keep.tile([P, T], U32, align_bytes=64)
        nc.sync.dma_start(x_word_table[:].bitcast(I32), x_words[0].rearrange("p n t -> p (n t)").bitcast(I32))
        x_scale_table = keep.tile([P, T], U8, align_bytes=64)
        for q in range(4):
            nc.sync.dma_start(
                x_scale_table[32 * q : 32 * q + 32, :].bitcast(I32),
                x_scales[0, 4 * q : 4 * q + 4, :].bitcast(I32).unsqueeze(0).to_broadcast([8, 4, T // 4]),
            )
        w_rows = w1.rearrange("(p j) c -> p j c", j=PACK)
        w_raw = []
        for u in range(2):
            w_half = keep.tile([P, PACK, H // 2], F32, name="w_half%d" % u)
            nc.sync.dma_start(w_half[:], w_rows[:, :, u * (H // 2) : (u + 1) * (H // 2)])
            w_raw.append(w_half)
            if u == 0:
                offs_list = load_list(offs, "offs_list")
        d_word_table = keep.tile([P, G], U32, align_bytes=64)
        nc.sync.dma_start(d_word_table[:].bitcast(I32), d_words[0].rearrange("p n t -> p (n t)").bitcast(I32))
        n2_list = load_list(n2, "n2_list")
        mem_rows = mem.rearrange("(b t r) w -> t b r w", t=PACK, r=RUN)
        pages = []
        for t in range(PACK):
            page = keep.tile([P, U], F32, name="page%d" % t)
            nc.sync.dma_start(page[:], mem_rows[t])
            pages.append(page)
        n1_list = load_list(n1, "n1_list")
        n3_list = load_list(n3, "n3_list")

        identity = keep.tile([P, P], F32)
        make_identity(nc, identity[:])
        weight_rows = keep.tile([P, P], F32)
        nc.gpsimd.memset(weight_rows[:], 0.0)
        for row, src in ((0, ga), (PACK, gb)):
            nc.gpsimd.dma_start(
                weight_rows[row : row + PACK, :], src.rearrange("(b t r) o -> t b (r o)", t=PACK, r=RUN)
            )
        weight_bank = psum.tile([P, P], F32, tag="second0")
        nc.tensor.transpose(weight_bank[:], weight_rows[:], identity[:])
        weight_cols = keep.tile([P, 2 * PACK], F32)
        nc.scalar.copy(weight_cols[:], weight_bank[:, : 2 * PACK])
        ga_cols = [weight_cols[:, t : t + 1] for t in range(PACK)]
        gb_cols = [weight_cols[:, PACK + t : PACK + t + 1] for t in range(PACK)]

        def gather(table, offsets, dtype, name, tag=None):
            picked = keep.tile([P, S], dtype, name=name, tag=tag or name, align_bytes=64)
            nc.vector.tensor_copy(picked[:], table[:].indirect(offsets[:]))
            return picked

        d_scales_picked = gather(d_scale_table, k1_list, U8, "d_scales_picked")
        d_scales_dealt = keep.tile([P, H], U8, align_bytes=64)
        nc.vector.tensor_copy(
            d_scales_dealt[:].bitcast(I32).rearrange("p (t b r) -> p b t r", t=PACK, r=RUN // 4),
            d_scales_picked[:].bitcast(I32).rearrange("p (b t r) -> p b t r", t=PACK, r=RUN // 4),
        )
        d_plane = keep.tile([P, H], U8, align_bytes=64)
        nc.vector.tensor_copy(d_plane[:].bitcast(I32), d_scales_dealt[:].bitcast(I32))
        for r in range(1, 4):
            nc.scalar.dma_start(d_plane[r:P:32, :].bitcast(I32), d_scales_dealt[8 * r : P : 32, :].bitcast(I32))
        two_words = gather(x_word_table, two_list, U32, "two_words")
        two_scales = gather(x_scale_table, two_list, U8, "two_scales")
        offs_words = gather(x_word_table, offs_list, U32, "offs_words")
        offs_scales = gather(x_scale_table, offs_list, U8, "offs_scales")

        w_grouped = keep.tile([P, PACK * H], BF16, tag="w_grouped", align_bytes=64)
        w_dealt = w_grouped[:].rearrange("p (t u b r j) -> p u b t r j", t=PACK, u=2, r=RUN, j=PACK)
        for u in range(2):
            nc.scalar.copy(w_dealt[:, u], w_raw[u][:].rearrange("p j (b t r) -> p b t r j", t=PACK, r=RUN))
        w_codes = keep.tile([P, H], U32, align_bytes=64)
        w_plane = keep.tile([P, H], U8, align_bytes=64)
        nc.vector.quantize_mx(out=w_codes[:].bitcast(FP8X4), scales=w_plane[:], in_=w_grouped[:])

        d_words_picked = gather(d_word_table, k1_list, U32, "d_words_picked", tag="w_grouped")
        d_codes = keep.tile([P, H], U32, align_bytes=64)
        nc.vector.tensor_copy(
            d_codes[:].rearrange("p (t b r) -> p b t r", t=PACK, r=RUN),
            d_words_picked[:].rearrange("p (b t r) -> p b t r", t=PACK, r=RUN),
        )

        def product(bank, codes, plane, t, moving_codes, moving_plane):
            cols = slice(t * P, (t + 1) * P)
            nc.tensor.matmul_mx(
                out=bank[:],
                lhsT=codes[:, cols].bitcast(FP8X4),
                lhsT_scale=plane[:, cols],
                rhs=moving_codes.bitcast(FP8X4),
                rhs_scale=moving_plane,
                start=True,
                stop=True,
            )

        b_rows = keep.tile([P, PACK, V], F32)
        for t in range(PACK):
            b_bank = psum.tile([P, BANK], F32, name="b_bank%d" % t, tag="first%d" % t)
            product(b_bank, w_codes, w_plane, t, two_words[:], two_scales[:])
            nc.scalar.copy(b_rows[:, t, :], b_bank[:])
        for t in range(PACK):
            nc.vector.tensor_copy(pages[t][:].indirect(n2_list[:]), b_rows[:, t, :])

        a_banks = []
        logs = []
        for t in range(PACK):
            a_bank = psum.tile([P, BANK], F32, name="a_bank%d" % t, tag="first%d" % t)
            product(a_bank, d_codes, d_plane, t, offs_words[:], offs_scales[:])
            log_tile = keep.tile([P, 2 * S], F32, name="log_tile%d" % t, tag="log%d" % t, align_bytes=64)
            nc.scalar.activation(log_tile[:, S:], a_bank[:], ACT.Abs)
            a_banks.append(a_bank)
            logs.append(log_tile)
        for t in range(PACK):
            nc.scalar.activation(logs[t][:, :S], logs[t][:, S:], ACT.Ln, bias=8.0)
        inverse = keep.tile([P, PACK, S], F32, tag="inverse", align_bytes=64)
        for t in range(PACK):
            nc.scalar.activation(inverse[:, t, :], logs[t][:].indirect(n1_list[:]), ACT.Exp, scale=-1.0)
        z_planes = keep.tile([P, PACK, S], BF16, align_bytes=64)
        for t in range(PACK):
            nc.vector.scalar_tensor_tensor(
                z_planes[:, t, :], a_banks[t][:], ga_cols[t], inverse[:, t, :], ALU.mult, ALU.mult
            )

        halves = [slice(h * BANK, (h + 1) * BANK) for h in range(2)]
        late_cols = keep.tile([P, 2 * PACK], F32, tag="log3", align_bytes=64)
        nc.scalar.copy(late_cols[:], weight_bank[:, : 2 * PACK])
        z2_grouped = [keep.tile([P, BANK, PACK], BF16, name="z2_grouped", tag="z2_grouped%d" % h, align_bytes=64) for h in range(2)]
        for t in range(PACK):
            for h in range(2):
                if t >= 2 and h == 1:
                    nc.scalar.activation(
                        z2_grouped[h][:, :, t], pages[t][:, halves[h]], ACT.Copy, scale=late_cols[:, PACK + t : PACK + t + 1]
                    )
                else:
                    nc.gpsimd.tensor_scalar(
                        z2_grouped[h][:, :, t], pages[t][:, halves[h]], gb_cols[t], 0.0, ALU.mult, ALU.add
                    )

        z_codes = keep.tile([P, S], U32, align_bytes=64)
        z_plane = keep.tile([P, S], U8, align_bytes=64)
        z_dealt = z_planes[:].rearrange("p t (b m r) -> p m b r t", m=PACK, r=RUN)

        def quantize_z(m, copy):
            cols = slice(m * P, (m + 1) * P)
            tag = "z_grouped%d" % m if m < 2 else "z2_grouped%d" % (m - 2)
            z_grouped = keep.tile([P, P * PACK], BF16, name="z_grouped", tag=tag, align_bytes=64)
            copy(z_grouped[:].rearrange("p (b r t) -> p b r t", r=RUN, t=PACK), z_dealt[:, m])
            nc.vector.quantize_mx(out=z_codes[:, cols].bitcast(FP8X4), scales=z_plane[:, cols], in_=z_grouped[:])

        z2_codes = keep.tile([P, U], U32, tag="inverse", align_bytes=64)
        z2_plane = keep.tile([P, U], U8, align_bytes=64)
        quantize_z(0, nc.vector.tensor_copy)
        for h in range(2):
            nc.vector.quantize_mx(
                out=z2_codes[:, halves[h]].bitcast(FP8X4),
                scales=z2_plane[:, halves[h]],
                in_=z2_grouped[h][:].rearrange("p c t -> p (c t)"),
            )
        quantize_z(1, nc.scalar.copy)

        out_rows = out.rearrange("(b m r) w -> m b r w", m=PACK, r=RUN)
        n3_halves = [n3_list[:, h * (BANK // 16) : (h + 1) * (BANK // 16)] for h in range(2)]
        s_banks = {}
        mixed = {}

        def first_step(m):
            half_s = ring.tile([P, U], F32, name="half_s")
            minus_s = ring.tile([P, U], F32, name="minus_s")
            for h in range(2):
                tag = ("second%d" if m < 2 else "first%d") % ((2 * m + h) % 4)
                s_banks[m, h] = psum.tile([P, BANK], F32, name="s_bank", tag=tag)
                product(s_banks[m, h], z_codes, z_plane, m, z2_codes[:, halves[h]], z2_plane[:, halves[h]])
                nc.scalar.activation(half_s[:, halves[h]], s_banks[m, h][:], ACT.Copy, scale=0.5 * 0.0625)
            for h in range(2):
                if m == 0 and h == 0:
                    nc.vector.tensor_scalar(minus_s[:, halves[h]], s_banks[m, h][:], -1.5 * 0.0625, None, ALU.mult)
                else:
                    nc.scalar.activation(minus_s[:, halves[h]], s_banks[m, h][:], ACT.Copy, scale=-1.5 * 0.0625)
            mixed[m] = ring.tile([P, U], F32, name="mixed")
            for h in range(2):
                nc.vector.tensor_tensor(
                    mixed[m][:, halves[h]], half_s[:].indirect(n3_halves[h]), minus_s[:, halves[h]], ALU.add
                )

        def second_step(m):
            s_rows = ring.tile([P, U], F32, name="s_rows")
            result = ring.tile([P, U], F32, name="result")
            for h in range(2):
                nc.scalar.activation(s_rows[:, halves[h]], s_banks[m, h][:], ACT.Copy, scale=0.0625)
                width = BANK // 2 if (m, h) == (PACK - 1, 1) else BANK
                for c in range(h * BANK, (h + 1) * BANK, width):
                    cols = slice(c, c + width)
                    offsets = n3_list[:, c // 16 : (c + width) // 16]
                    nc.vector.tensor_tensor(result[:, cols], mixed[m][:].indirect(offsets), s_rows[:, cols], ALU.add)
                    nc.sync.dma_start(out_rows[m][:, :, cols], result[:, cols])

        first_step(0)
        for m in range(1, PACK):
            first_step(m)
            if m == 1:
                quantize_z(2, nc.scalar.copy)
                quantize_z(3, nc.scalar.copy)
            second_step(m - 1)
        second_step(PACK - 1)
